import numpy as np, ml_dtypes
CORES = [2,3,42,43,82,83,122,123]
N = 8
BF = ml_dtypes.bfloat16
def gentries(a):
    return np.ascontiguousarray(a.reshape(8, 16, -1).transpose(0, 2, 1)).reshape(8, -1)
def gtable(e):
    e = np.asarray(e); return np.ascontiguousarray(e.reshape(8, -1, 16).transpose(0, 2, 1)).reshape(128, -1).astype(np.int32)
V, G, CAP, RO = 1536, 224, 384, 3
W = V + (N - 1) * G + 17
H = 16 - RO
def parts(rng):
    h = V // 2; S = (N, 8, 16, V)
    o = np.argsort(rng.random(S), axis=-1); a, b = o[..., :h], o[..., h:]
    pool = np.concatenate([b, np.broadcast_to(np.arange(V, W), (N, 8, 16, W - V))], axis=-1)
    pool = np.take_along_axis(pool, np.argsort(rng.random(pool.shape), axis=-1), -1)[..., :V - h]
    nb = np.zeros(S, np.int64)
    np.put_along_axis(nb, o, np.concatenate([a.reshape(N, 8, 16, h // 2, 2)[..., ::-1].reshape(N, 8, 16, h), pool], axis=-1), -1)
    share = rng.permutation(np.array([0.003, 0.003, 0.01, 0.02, 0.05, 0.1, 0.3, 0.6])).reshape(1, 8, 1, 1) * np.exp2(rng.integers(-1, 2, (N, 8, 1, 1)))
    m = (rng.random((N, 8, 1, V)) < share) & (rng.random(S) < 0.5)
    d0 = np.where(m, rng.integers(0, 201, S), 255); nd = rng.integers(1, 64, S); e = rng.random(S)
    lab = np.where(e < 0.3, W - 1, np.where(e < 0.5, rng.integers(W - 17, W - 1, S), rng.integers(0, W - 17, S)))
    hi = rng.permuted(np.tile(np.array([8, 16, 32, 64, 96, 128, 192, 256]), (N, 1)), axis=1).reshape(N, 8, 1, 1)
    ld = (rng.random(S) * hi).astype(np.int64)
    rt = rng.integers(20, 181, (8, 16, 16)); rt[:, np.arange(16), np.arange(16)] = 0; rt = np.tile(rt, (N, 1, 1, 1))
    p = rng.permuted(np.tile(np.array([0.03, 0.05, 0.1, 0.15, 0.2, 0.3, 0.5, 1.0]), (N, 1)), axis=1).reshape(N, 8, 1)
    fl = (rng.random((N, 8, V)) < p).astype(np.int64)
    snd = np.ascontiguousarray(np.argsort(rng.random((N, 8, N - 1, V)), axis=-1)[..., :G])
    return nb, nd, lab, ld, d0, rt, fl, snd
def flat(a, t):
    return np.ascontiguousarray(a.reshape(N, 128, -1)).astype(np.float32).astype(t)
def pack(nb, nd, lab, ld, d0, rt, fl, snd):
    lab = np.array(lab); ld = np.array(ld); lab[:, :, H:] = W - 1; ld[:, :, H:] = 255
    return {"nb": flat(nb, np.int32), "nd": flat(nd, BF), "lab": flat(lab, np.int32), "ld": flat(ld, BF), "d0": flat(d0, BF), "rt": flat(rt, BF),
            "fl": fl.astype(np.int32), "snd": np.stack([gtable(a.reshape(8, -1)) for a in snd])}
def put(row, j, p):
    old = int(row[j]); row[row == p] = old; row[j] = p
def load(rng, nq, nl, lq, dq, fq, sq):
    s = np.nonzero(fq)[0][:CAP]; t = rng.permutation(np.setdiff1d(np.arange(V), s)); T = (N - 1) * G
    sq[:] = rng.permutation(np.concatenate([rng.permutation(s), t])[:G])
    nq[0, s] = t[:CAP]; nq[0, t] = rng.permutation(np.concatenate([t[CAP:], s])); gp = V + rng.permutation(T)
    for i in range(1, 16):
        p = gp[(np.arange(CAP) + (i - 1) * CAP) % T]
        nq[i, s] = p; nq[i, t] = rng.permutation(np.setdiff1d(np.arange(W), p))[:V - CAP]
    nl[:, s] = rng.integers(1, 50, (16, CAP)); lq[:] = W - 1
    dq[:] = 255; dq[:, t[:CAP]] = rng.integers(0, 101, (16, CAP))
def setup_inputs(rng):
    return pack(*parts(rng))
def setup_inputs_room(rng):
    nb, nd, lab, ld, d0, rt, fl, snd = parts(rng); fl[:] = 0
    for q in range(N):
        full = q >= max(1, N // 4)
        for g in range(8):
            n = int(rng.choice(np.array([CAP, CAP + 1, V] if full else [0, 1, CAP - 1, CAP, CAP + 1, V])))
            if q == 0: n = (CAP, CAP + 1, CAP - 1, V, 0, 1, CAP, CAP + 1)[g]
            fl[q, g, rng.permutation(V)[:n]] = 1
            if full: load(rng, nb[q, g], nd[q, g], lab[q, g], d0[q, g], fl[q, g], snd[q, g])
    c = snd[0, 0, 0]; isin = np.zeros(V, np.int64); isin[c] = 1
    o = np.concatenate([rng.permutation(c), rng.permutation(np.nonzero(isin == 0)[0])])
    s, t = o[:CAP], rng.permutation(o[CAP:])
    fl[0, 0] = 0; fl[0, 0, s] = 1
    nb[0, 0, 0, s] = t[:CAP]; nb[0, 0, 0, t] = rng.permutation(np.concatenate([t[CAP:], s]))
    nd[0, 0][:, s] = rng.integers(1, 50, (16, CAP)); lab[0, 0][:, s] = W - 1
    d0[0, 0][:, s] = 255; d0[0, 0][:, t[:CAP]] = rng.integers(0, 101, (16, CAP))
    return pack(nb, nd, lab, ld, d0, rt, fl, snd)
def setup_inputs_ties(rng):
    nb, nd, lab, ld, d0, rt, fl, snd = parts(rng); S = (N, 8, 16, V)
    base = np.array([0, 0, 1, 4, 250, 251, 252, 252]).reshape(1, 8, 1, 1); share = np.array([0.3, 0.1, 0.02, 0.3, 0.02, 0.02, 0.01, 0.005]).reshape(1, 8, 1, 1)
    m = (rng.random((N, 8, 1, V)) < share) & (rng.random(S) < 0.6)
    d0 = np.where(m, base + rng.integers(0, 4, S), 255); nd = rng.integers(0, 3, S); ld = rng.integers(0, 4, S)
    rt = np.minimum(base + rng.integers(0, 5, (N, 8, 16, 16)), 255)
    return pack(nb, nd, lab, ld, d0, rt, fl, snd)
def setup_inputs_alike(rng):
    nb, nd, lab, ld, d0, rt, fl, snd = parts(rng)
    q = int(rng.integers(0, N)); o = rng.permutation(CAP)[:12]; u, x = o[:4], o[4:8]
    for a in range(N):
        d = (a - q) % N; v = o[8:]; p = u
        if d > 0:
            v = rng.permutation(CAP)[:4]; sp = rng.permutation(G)[:4]; p = V + (d - 1) * G + sp
            for j in range(4): put(snd[q, 0, d - 1], sp[j], u[j])
        for j in range(4): put(nb[a, 0, 0], v[j], p[j])
        nd[a, 0][:, v] = rng.integers(1, 50, (16, 4)); lab[a, 0][:, v] = W - 1; d0[a, 0][:, v] = 255; fl[a, 0, v] = 1
    for j in range(4): put(nb[q, 0, 0], u[j], x[j])
    nd[q, 0][:, u] = rng.integers(1, 30, (16, 4)); lab[q, 0][:, u] = W - 1; fl[q, 0, u] = 0
    d0[q, 0][:, u] = rng.integers(60, 101, (16, 4)); d0[q, 0][:, x] = 0
    nb[:, 0] = np.array(nb[:, 0, :1]); nb[:, 1, 0] = np.arange(V); nb[:, 2] = W - 1 - np.arange(V); nb[:, 3] = np.arange(V, 2 * V)
    lab[:, 4] = rng.choice(np.array([0, V - 1, V, W - 18, W - 17, W - 2, W - 1]), (N, 16, V)); lab[:, 5] = np.array(lab[:, 5, :1])
    snd[:, 1::2] = np.array(snd[:, 1::2, :1])
    return pack(nb, nd, lab, ld, d0, rt, fl, snd)
def setup_inputs_quiet(rng):
    nb, nd, lab, ld, d0, rt, fl, snd = parts(rng)
    q = int(rng.integers(0, N)); g = rng.permutation(8); w = fl[q] * 1; fl[:] = 0; fl[q] = w
    fl[q, g[0]] = 0; fl[q, g[1]] = 0; fl[q, g[1], 0] = 1; fl[q, g[1], V - 1] = 1
    h = int(g[2]); fl[q, h] = 1
    for i in range(16):
        p = rng.permutation(CAP) if i == 0 else CAP + rng.permutation(V - CAP)[:CAP]
        nb[q, h, i, :CAP] = p; nb[q, h, i, CAP:] = rng.permutation(np.setdiff1d(np.arange(W), p))[:V - CAP]
    nd[q, h][:, :CAP] = 255; nd[q, h, 1, :CAP] = rng.integers(1, 50, CAP); lab[q, h][:, :CAP + 8] = W - 1
    d0[q, h][:, :CAP] = 255; d0[q, h][:, CAP:] = rng.integers(50, 101, (16, V - CAP)); d0[q, h][:, V - 8:] = 0
    for j in range(8): put(nb[q, h, 0], CAP + j, V - 8 + j)
    nd[q, h, 0, CAP:CAP + 8] = rng.integers(1, 30, 8)
    return pack(nb, nd, lab, ld, d0, rt, fl, snd)
def setup_inputs_spread(rng):
    nb, nd, lab, ld, d0, rt, fl, snd = parts(rng); S = (N, 8, 16, V)
    d0 = np.where(rng.random((N, 8, 1, V)) < 0.2, 255, np.minimum(np.exp2(8 * rng.random((N, 8, 1, V))) * (0.5 + rng.random(S)), 255).astype(np.int64))
    nd = np.minimum(np.exp2(8.1 * rng.random(S)).astype(np.int64) - (rng.random(S) < 0.5), 255)
    ld = np.minimum(np.exp2(8.1 * rng.random(S)).astype(np.int64), 255) * (rng.random(S) < 0.97)
    lab = rng.integers(0, W, S); rt = rng.integers(0, 256, (N, 8, 16, 16))
    fl = (rng.random((N, 8, V)) < rng.random((N, 8, 1)) * rng.random((N, 8, V))).astype(np.int64)
    return pack(nb, nd, lab, ld, d0, rt, fl, snd)
def check_inputs(d):
    bad = []
    for k, lo, hi in (("nb", 0, W - 1), ("lab", 0, W - 1), ("fl", 0, 1), ("snd", 0, V - 1)):
        if np.min(d[k]) < lo or np.max(d[k]) > hi: bad.append("range of " + k)
    for k in ("nd", "ld", "d0", "rt"):
        a = np.asarray(d[k]).astype(np.float32)
        if not np.all((a >= 0) & (a <= 255) & (a == np.floor(a))): bad.append("whole numbers from 0 to 255 in " + k)
    if np.any(np.diff(np.sort(np.asarray(d["nb"]), axis=-1), axis=-1) == 0): bad.append("nb: the numbers of one row differ")
    s = np.stack([gentries(a) for a in np.asarray(d["snd"])]).reshape(N, 8, N - 1, G)
    if np.any(np.diff(np.sort(s, axis=-1), axis=-1) == 0): bad.append("snd: the numbers of one block differ")
    if np.any(np.asarray(d["lab"]).reshape(N, 8, 16, V)[:, :, H:] != W - 1): bad.append("lab: the later entries are the none place")
    if np.any(np.asarray(d["ld"]).astype(np.float32).reshape(N, 8, 16, V)[:, :, H:] != 255): bad.append("ld: the later entries are 255")
    return bad
def ints(a):
    return np.asarray(a).astype(np.float32).astype(np.int64)
def reference(nb, nd, lab, ld, d0, rt, fl, snd):
    S = (N, 8, 16, V); nbl = ints(nb).reshape(S); ndl = ints(nd).reshape(S)
    L = np.array(ints(lab).reshape(S)); M = np.array(ints(ld).reshape(S)); D = np.array(ints(d0).reshape(S))
    R = ints(rt).reshape(N, 8, 16, 16); flag = ints(fl).reshape(N, 8, V) > 0
    sl = np.stack([gentries(a) for a in snd]).astype(np.int64).reshape(N, 8, N - 1, G)
    none = np.full((8, 16, 1), 255, np.int64)
    for t in range(RO):
        F = flag & (np.add.accumulate(flag.astype(np.int64), axis=2) <= CAP)
        flag = flag & ~F
        new = np.array(D); push = np.zeros((N, 8, W), bool)
        for a in range(N):
            guests = [np.take_along_axis(D[(a - d) % N], sl[(a - d) % N, :, d - 1][:, None, :], 2) for d in range(1, N)]
            win = np.concatenate([D[a]] + guests + [R[a], none], axis=2)
            for g in range(8):
                v = np.nonzero(F[a, g])[0]; w = win[g]; old = D[a, g][:, v]
                cand = np.minimum(np.min(w[:, nbl[a, g][:, v]] + ndl[a, g][:, v], axis=1), 255)
                q = np.minimum(np.min(w[:, L[a, g][:, v]] + M[a, g][:, v], axis=1), 255)
                up = (cand < q) & (cand < old); ch = np.any(up, axis=0)
                key = np.where(up, cand, 1000); best = np.argmin(key, axis=0); least = np.min(key, axis=0)
                new[a, g][:, v] = np.where(up, cand, old)
                L[a, g, H + t, v[ch]] = W - 17 + best[ch]; M[a, g, H + t, v[ch]] = least[ch]
                push[a, g, nbl[a, g][:, v[ch]]] = True
        D = new
        for a in range(N):
            flag[a] |= push[a, :, :V]
            for d in range(1, N):
                back = np.zeros((8, V), bool)
                np.put_along_axis(back, sl[(a - d) % N, :, d - 1], push[a, :, V + (d - 1) * G:V + d * G], 1)
                flag[(a - d) % N] |= back
    return {"yd": D.reshape(N, 128, V).astype(np.float32).astype(BF), "yl": L.reshape(N, 128, V).astype(np.float32)}

from concourse.mybir import AluOpType, ActivationFunctionType
from concourse.bass import DstId, RemoteDMATransfer

A = AluOpType
F = ActivationFunctionType
V, GS, CAP, RO, NR = 1536, 224, 384, 3, 8
NG = (NR - 1) * GS
NONE = V + NG + 16
WW = NONE + 16
VP = V + CAP
FWW = WW + CAP
UC = 64
NU = CAP // UC
VUNITS = 3
VPUSH = 7
VBACK = 3
VCOL = 48
FV = 32.0
THR = 30 * FV + FV / 2

f32, b16, i32, u16 = "float32", "bfloat16", "int32", "uint16"


def sb(n, t):
    return ("sbuf", [128, n], t)


SCRATCH = {
    "w0": sb(WW, b16), "w1": sb(WW, b16), "w2": sb(WW, b16), "dm": sb(VP, b16),
    "nbi": sb(VP, i32), "labi": sb(V, i32), "labf": sb(VP, f32), "zt": sb(VP, f32),
    "ndt": sb(VP, b16), "lda": sb(VP, b16), "ldb": sb(VP, b16),
    "sndi": sb(98, i32), "sndu": sb(98, u16), "sndf": sb(98, f32),
    "fli": ("sbuf", [128, 3, 32], i32), "flf": sb(96, b16), "fz": sb(112, b16),
    "sd0": sb(NG, b16), "sd1": sb(NG, b16), "sd2": sb(NG, b16),
    "fs0": sb(98, b16), "fs1": sb(98, b16), "fr0": sb(98, b16), "fr1": sb(98, b16),
    "bo": sb(98, f32), "bu": sb(98, u16),
    "fv": sb(FWW, b16), "fa": sb(FWW, f32),
    "ex": sb(16 + NG, f32), "t1": sb(98, f32), "thr": sb(96, f32), "ta": sb(96, f32), "tb": sb(96, f32),
    "dum": sb(96, f32), "nf": sb(96, f32), "nfd": sb(96, f32), "cum": sb(96, f32), "off": sb(96, f32),
    "offu": sb(96, u16), "z96": sb(96, b16),
    "pay": sb(VP, f32), "ya": sb(3200, f32), "yb": sb(3200, f32), "ym": sb(CAP, f32), "yh": sb(CAP, f32),
    "c16": sb(CAP, f32), "hold": sb(CAP, f32), "ids": sb(24, u16),
    "nbu": sb(CAP, u16), "labu": sb(CAP, u16), "nbf": sb(CAP, f32), "labt": sb(CAP, f32),
    "rn": sb(2 * CAP, b16), "rl": sb(2 * CAP, b16),
    "gn": sb(16 * CAP, b16), "gl": sb(16 * CAP, b16), "on": sb(16 * CAP, b16), "ol": sb(16 * CAP, b16),
    "up": sb(CAP, b16), "xx": sb(CAP + 16, f32), "tx": sb(2 * CAP, f32), "lst": sb(CAP, u16), "sl": sb(24, u16),
    "newd": sb(CAP, b16), "kt": sb(CAP, f32), "ks": sb(CAP, f32), "kd": sb(CAP, b16),
    "ki": sb(24, i32), "km": sb(24, i32), "kc": sb(24, i32), "kh": sb(24, f32), "kf": sb(24, f32),
    "zl": sb(CAP, f32), "zd": sb(CAP, b16), "dl": sb(CAP, f32), "dd": sb(CAP, b16),
    "cvb": sb(CAP, b16), "caf": sb(CAP, f32),
    "one": sb(128, b16), "bk0": sb(128, b16), "bk": sb(128, b16), "tri": sb(128, b16), "ust": sb(128, b16),
    "idn": sb(128, b16), "nid": sb(128, b16), "nbk": sb(128, b16), "dmx": sb(9 * 128, b16),
    "ra": sb(CAP, b16), "rb": sb(CAP, b16), "rc": sb(CAP, b16),
    "paf": sb(V, f32), "pab": sb(V, b16),
    "pp": sb(24, i32), "s1": sb(24, i32), "s2": sb(24, f32), "s3": sb(24, i32),
    "s4": sb(24, f32), "s5": sb(24, f32), "s6": sb(24, f32),
    "rr": sb(4, i32), "rf": sb(4, f32), "e8": sb(8, f32), "wt": sb(12, f32), "mk": sb(4, f32),
    "pd": ("psum", [128, 2048], f32), "pc": ("psum", [128, 512], f32), "pk": ("psum", [128, 512], f32),
    "pv": ("psum", [128, 512], f32), "pq": ("psum", [128, 512], f32),
}
NDMA = 60
SEMAPHORES = ["cv", "cs", "ct", "cg", "ad0", "ad1", "ad2", "af0", "af1", "ld0", "ld1", "ld2", "lf0", "lf1"] + \
             ["d%d" % k for k in range(NDMA)]


def engine_plan(topo, cores, src):
    far, plane, near = [], [], []
    for c in cores:
        if c == src:
            continue
        if topo.chip(c) == topo.chip(src):
            near.append(c)
        elif topo.same_plane(topo.chip(c), topo.chip(src)):
            plane.append(c)
        else:
            far.append(c)
    plan = {}
    out = topo.engines(src, (far + plane)[0])
    for call, grp in ((0, far), (1, plane)):
        k = len(out) // len(grp)
        for j, c in enumerate(grp):
            plan[c] = (call, out[j * k:(j + 1) * k])
    for c in near:
        plan[c] = (1, [e for e in topo.engines(src, c) if e not in out])
    return plan


def rank_program(g, core, T, topo):
    rank = T.rank_of(core)
    if rank is None:
        return
    S = T.sem
    cores = list(T.cores)
    Q = {"g": g, "v": g.vector, "s": g.scalar, "t": g.tensor, "y": g.sync}
    CS = {"g": "cg", "v": "cv", "s": "cs", "t": "ct"}
    cnt = {}
    known = {q: {} for q in Q}
    lastw, readers, excl = {}, {}, {}
    nd = [0]

    def need(q, ev):
        sem, val, clock = ev[0], ev[1], ev[2]
        if known[q].get(sem, 0) >= val:
            return
        Q[q].wait_ge(S[sem], val)
        known[q][sem] = val
        for k, x in clock.items():
            if known[q].get(k, 0) < x:
                known[q][k] = x

    def order(q, R, W, X):
        evs = []
        for k in R:
            evs += lastw.get(k, [])
        for k in W:
            evs += lastw.get(k, []) + readers.get(k, [])
        for k in X:
            if k in excl and excl[k][3] != q:
                evs.append(excl[k])
        top = {}
        for ev in evs:
            if ev[0] not in top or top[ev[0]][1] < ev[1]:
                top[ev[0]] = ev
        for ev in top.values():
            need(q, ev)

    def record(ev, R, W, X):
        for k in R:
            readers.setdefault(k, []).append(ev)
        for k in W:
            lastw[k] = [ev]
            readers[k] = []
        for k in X:
            excl[k] = ev

    def op(q, make, R=(), W=(), X=()):
        order(q, R, W, X)
        sem = CS[q]
        make().then_inc(S[sem], 1)
        cnt[sem] = cnt.get(sem, 0) + 1
        record((sem, cnt[sem], dict(known[q]), q), R, W, X)

    def dma(q, out, in_, R=(), W=()):
        order(q, R, W, ())
        sem = "d%d" % nd[0]
        nd[0] += 1
        Q[q].dma_start(out, in_).then_inc(S[sem], 16)
        cnt[sem] = 16
        record((sem, 16, dict(known[q]), "dma"), R, W, ())

    plans = {c: engine_plan(topo, cores, c) for c in cores}

    def exchange(src, dst, sign, arr, loc, R, W):
        order("g", R, (), ())
        tot = 0
        for call in (0, 1):
            tr = []
            for d in range(1, NR):
                c = cores[(rank + sign * d) % NR]
                k, eng = plans[core][c]
                if k != call:
                    continue
                rid, pid, se = topo.addr(c)
                m = 0
                for e in eng:
                    m |= 1 << e
                tr.append(RemoteDMATransfer(dst_ids=[DstId(rid=rid, pnc=pid)], dma_engine_mask=m, remote_sem=S[arr],
                                            src=src(d), dst=dst(d)))
                tot += len(eng)
            g.remote_dma_fused(tr, local_sem=S[loc])
        cnt[loc] = tot
        record((loc, tot, dict(known["g"]), "dma"), R, (), ())
        n_in = sum(len(plans[c][core][1]) for c in cores if c != core)
        cnt[arr] = n_in
        record((arr, n_in, {}, "dma"), (), W, ())

    v, s, t = g.vector, g.scalar, g.tensor
    W_ = [T.w0, T.w1, T.w2]
    SD = [T.sd0, T.sd1, T.sd2]
    FS, FR = [T.fs0, T.fs1], [T.fr0, T.fr1]
    fv, fa = T.fv, T.fa
    kv, ka = ["fv%d" % j for j in range(3)], ["fa%d" % j for j in range(3)]

    def fill(ap, c, key):
        op("v", lambda: v.memset(ap, c), W=[key])

    def gio(ap, pat, base, cm, key, fl=True):
        if fl:
            op("g", lambda: g.iota(ap, pat, base, cm, allow_small_or_imprecise_dtypes=True), W=[key])
        else:
            op("g", lambda: g.iota(ap, pat, base, cm), W=[key])

    def ts(out, in0, s1, s2, o0, o1, R, W, X=()):
        if o1 is None:
            op("v", lambda: v.tensor_scalar(out, in0, s1, None, o0), R, W, X)
        else:
            op("v", lambda: v.tensor_scalar(out, in0, s1, s2, o0, o1), R, W, X)

    def tt(out, a, b, o, R, W, X=()):
        op("v", lambda: v.tensor_tensor(out, a, b, o), R, W, X)

    def cp(out, a, R, W, X=()):
        op("v", lambda: v.tensor_copy(out, a), R, W, X)

    def scan(out, a, b, init, o0, o1, R, W, X=()):
        op("v", lambda: v.tensor_tensor_scan(out, a, b, init, o0, o1), R, W, X)

    def tr32(out, a, R, W, X=()):
        op("v", lambda: v.transpose(out, a), R, W, X)

    def act(out, a, fn, R, W, **kw):
        op("s", lambda: s.activation(out, a, fn, **kw), R, W)

    def mm(out, l, r, st, sp, R, X):
        op("t", lambda: t.matmul(out, l, r, st, sp), R, (), X)

    dma("y", T.sndi[:], T.snd[:], W=["sndi"])
    dma("y", T.w0[:, 0:V], T.d0[:], W=["w0o"])
    for h in range(2):
        dma("y", T.fli[:, :, 16 * h:16 * h + 16], T.fl[h:8:2, :], W=["fli%d" % h])
    dma("y", T.nbi[:, 0:V], T.nb[:], W=["nbi"])
    dma("y", T.ndt[:, 0:V], T.nd[:], W=["ndt"])
    dma("y", T.labi[:], T.lab[:], W=["labi"])
    dma("y", T.lda[:, 0:V], T.ld[:], W=["lda"])
    dma("y", T.w0[:, V + NG:NONE], T.rt[:], W=["w0r"])

    fill(T.one[:], 1.0, "one")
    gio(T.pay[:, 0:CAP], [[1, CAP]], 0, 0, "pay0")
    gio(T.pp[:], [[16, 24]], 0, 1, "pp", False)
    op("g", lambda: g.affine_select(T.bk0[:], T.one[:], [[-16, 8], [0, 16]], A.is_ge, 0.0, 0, 1), ["one"], ["bk0"])
    op("g", lambda: g.affine_select(T.bk[:], T.bk0[:], [[16, 8], [0, 16]], A.is_ge, 0.0, 15, -1), ["bk0"], ["bk"])
    op("g", lambda: g.affine_select(T.tri[:], T.bk[:], [[1, 128]], A.is_ge, 0.0, 0, -1), ["bk"], ["tri"])
    op("g", lambda: g.affine_select(T.ust[:], T.bk[:], [[-1, 128]], A.is_gt, 0.0, 0, 1), ["bk"], ["ust"])
    gio(T.dum[:], [[16, 96]], V, 1, "dum")
    gio(T.c16[:], [[0, 24], [1, 16]], 0, 0, "c16")
    act(T.yb[:, 0:CAP], T.pay[:, 0:CAP], F.Silu, ["pay0"], ["yb"], bias=float(V))
    for k in range(1, 5):
        act(T.pay[:, k * CAP:(k + 1) * CAP], T.pay[:, 0:CAP], F.Identity, ["pay0"], ["pay%d" % k], bias=float(k * CAP))
    act(T.ya[:, 0:CAP], T.pay[:, 0:CAP], F.Identity, ["pay0"], ["ya"], bias=float(V))
    PAY = ["pay%d" % k for k in range(5)]
    fill(T.fz[:, 0:16], 0.0, "fz0")
    fill(T.z96[:], 0.0, "z96")
    fill(T.nbi[:, V:VP], NONE, "nbp")
    fill(T.ndt[:, V:VP], 255.0, "ndp")
    fill(T.lda[:, V:VP], 255.0, "ldap")
    fill(T.labf[:, V:VP], float(NONE), "labp")
    fill(T.w0[:, NONE:WW], 255.0, "w0n")
    op("v", lambda: v.memset(T.pd[:, 0:2048:16], 1024.0), X=["pd0", "pd1"])
    ts(T.rr[:, 0:1], T.pp[:, 0:1], 15, None, A.bitwise_and, None, ["pp"], ["rr0"])
    ts(T.rr[:, 1:2], T.pp[:, 0:1], 7, None, A.bitwise_and, None, ["pp"], ["rr1"])
    ts(T.rr[:, 2:3], T.pp[:, 0:1], 16, None, A.bitwise_and, None, ["pp"], ["rr2"])
    cp(T.rf[:, 0:3], T.rr[:, 0:3], ["rr0", "rr1", "rr2"], ["rf"])
    ts(T.e8[:], T.pay[:, 0:8], T.rf[:, 1:2], None, A.is_equal, None, ["pay0", "rf"], ["e8"])
    ts(T.mk[:, 0:1], T.rf[:, 0:1], 7.5, None, A.is_lt, None, ["rf"], ["mk0"])
    ts(T.mk[:, 1:2], T.rf[:, 0:1], 7.5, None, A.is_gt, None, ["rf"], ["mk1"])
    ts(T.mk[:, 2:3], T.rf[:, 0:1], 14.5, T.mk[:, 1:2], A.is_lt, A.mult, ["rf", "mk1"], ["mk2"])
    tt(T.wt[:, 1:8], T.e8[:, 0:7], T.e8[:, 1:8], A.subtract, ["e8"], ["wt1"])
    ts(T.wt[:, 0:1], T.e8[:, 0:1], -1.0, None, A.mult, None, ["e8"], ["wt0"])
    cp(T.wt[:, 8:9], T.e8[:, 7:8], ["e8"], ["wt8"])

    cp(T.sndu[:], T.sndi[:], ["sndi"], ["sndu"])
    hv = 4 * GS
    cp(T.sd0[:, 0:hv], T.w0[:, 0:V].indirect(T.sndu[:, 0:hv // 16]), ["w0o", "sndu"], ["sd0a"])
    act(T.sd0[:, hv:NG], T.w0[:, 0:V].indirect(T.sndu[:, hv // 16:98]), F.Copy, ["w0o", "sndu"], ["sd0b"])

    def send_d(r, R):
        exchange(lambda d: SD[r][:, (d - 1) * GS:d * GS], lambda d: W_[r][:, V + (d - 1) * GS:V + d * GS], 1,
                 "ad%d" % r, "ld%d" % r, R, ["w%dg" % r])

    send_d(0, ["sd0a", "sd0b"])

    for b in range(3):
        cp(T.flf[:, 32 * b:32 * b + 32], T.fli[:, b, :], ["fli0", "fli1"], ["flf%d" % b])
    for b in range(3):
        tr32(T.fz[:, 16 + b:112:3], T.flf[:, 32 * b:32 * b + 32], ["flf%d" % b], ["f%d" % b])
    FK = ["f0", "f1", "f2"]
    ts(T.hold[:], T.c16[:], T.rf[:, 0:1], 4096.0, A.is_le, A.mult, ["c16", "rf"], ["hold"])
    for j in range(9):
        act(T.dmx[:, 128 * j:128 * j + 128], T.bk[:], F.Identity, ["bk", "wt0", "wt1", "wt8"], ["dm%d" % j],
            scale=T.wt[:, j:j + 1])
    DM = ["dm%d" % j for j in range(9)]

    def late_constants():
        op("g", lambda: g.affine_select(T.idn[:], T.one[:], [[-1, 128]], A.is_equal, 0.0, 0, 1), ["one"], ["idn"])
        gio(T.ra[:], [[128, 3], [0, 128]], WW, 0, "ra")
        gio(T.rb[:], [[0, 3], [1, 128]], 0, 0, "rb")
        gio(T.rc[:], [[0, CAP]], 4096, 0, "rc")
        gio(T.cvb[:], [[0, CAP]], int(FV), 0, "cvb")
        gio(T.caf[:], [[0, CAP]], int(FV), 0, "caf")
        gio(T.zl[:], [[0, CAP]], 0, 0, "zl")
        gio(T.zd[:], [[0, CAP]], 0, 0, "zd")
        gio(T.ex[:, 0:16], [[0, 16]], 0, 0, "ex0")
        gio(T.ldb[:, V:VP], [[0, CAP]], 255, 0, "ldbp")
        gio(T.dm[:, V:VP], [[0, CAP]], 255, 0, "dmp")
        gio(T.w1[:, NONE:WW], [[0, 16]], 255, 0, "w1n")
        gio(T.w2[:, NONE:WW], [[0, 16]], 255, 0, "w2n")
        gio(T.zt[:], [[0, VP]], NONE, 0, "zt")

    def late_vector():
        ts(T.paf[:, 0:CAP], T.c16[:], T.rf[:, 0:1], FV, A.not_equal, A.mult, ["c16", "rf"], ["paf"])
        ts(T.pab[:, 0:CAP], T.c16[:], T.rf[:, 0:1], FV, A.not_equal, A.mult, ["c16", "rf"], ["pab"])
        ts(T.nid[:], T.idn[:], -4096.0, None, A.mult, None, ["idn"], ["nid"])
        ts(T.nbk[:], T.bk[:], -4096.0, None, A.mult, None, ["bk"], ["nbk"])
        cp(T.sndf[:], T.sndi[:], ["sndi"], ["sndf"])
        fill(T.kd[:], -0.0625, "kd")
        ts(T.s1[:], T.pp[:], T.rf[:, 0:1], None, A.add, None, ["pp", "rf"], ["s1"])
        cp(T.s6[:, 0:1], T.pp[:, 0:1], ["pp"], ["s6"])
        fill(T.kd[:, 0:CAP:16], 8192.0, "kd")
        ts(T.s2[:], T.s1[:], T.s6[:, 0:1], None, A.subtract, None, ["s1", "s6"], ["s2"])
        ts(T.s3[:], T.s2[:], -11.5, 1.0 / 24, A.add, A.mult, ["s2"], ["s3"])
        ts(T.s5[:], T.s2[:], 32.0, None, A.mult, None, ["s2"], ["s5"])
        ts(T.s4[:], T.s3[:], -767.0, T.rf[:, 2:3], A.mult, A.add, ["s3", "rf"], ["s4"])
        tt(T.s2[:], T.s4[:], T.s5[:], A.add, ["s4", "s5"], ["s2"])
        cp(T.sl[:], T.s2[:], ["s2"], ["sl"])

    def clear_flags():
        for j, (a, b) in enumerate(((0, V), (V, 2 * V), (2 * V, WW))):
            dma("y", fa[:, a:b], T.paf[:, 0:b - a], ["paf"], [ka[j]])
            dma("y", fv[:, a:b], T.pab[:, 0:b - a], ["pab"], [kv[j]])

    def late_dmas():
        for n in (CAP, 2 * CAP):
            dma("y", T.paf[:, n:2 * n], T.paf[:, 0:n], ["paf"], ["paf"])
            dma("y", T.pab[:, n:2 * n], T.pab[:, 0:n], ["pab"], ["pab"])
        clear_flags()
        dma("y", T.dm[:, 0:V], T.d0[:], W=["dm"])
        dma("y", T.ldb[:, 0:V], T.ld[:], W=["ldb"])
        dma("y", T.w1[:, V + NG:NONE], T.rt[:], W=["w1r"])
        dma("y", T.w2[:, V + NG:NONE], T.rt[:], W=["w2r"])

    f_ = T.fz[:, 16:112]
    for r in range(RO):
        last = r == RO - 1
        w = W_[r]
        WK = ["w%do" % r, "w%dg" % r, "w%dr" % r, "w%dn" % r]
        mm(T.pq[:, 0:96], T.tri[:], f_, True, False, FK + ["tri"], ["pq"])
        mm(T.pq[:, 0:96], T.ust[:], T.fz[:, 15:111], False, True, FK + ["fz0", "ust"], ["pq"])
        ts(T.nf[:], f_, -4096.0, None, A.mult, None, FK, ["nf"])
        scan(T.cum[:], T.pq[:, 0:96], T.z96[:], -1.0, A.add, A.add, ["z96"], ["cum"], ["pq"])
        tt(T.nfd[:], T.nf[:], T.dum[:], A.add, ["nf", "dum"], ["nfd"])
        tt(T.off[:], T.cum[:], T.nfd[:], A.max, ["cum", "nfd"], ["off"])
        cp(T.offu[:], T.off[:], ["off"], ["offu"])
        act(T.yb[:].indirect(T.offu[:, VCOL:96]), T.pay[:, 16 * VCOL:V], F.Silu, PAY + ["offu"], ["yb"])
        cp(T.ya[:].indirect(T.offu[:, 0:VCOL]), T.pay[:, 0:16 * VCOL], PAY + ["offu"], ["ya"])
        tt(T.ym[:], T.ya[:, 0:CAP], T.yb[:, 0:CAP], A.min, ["ya", "yb"], ["ym"])
        scan(T.yh[:], T.hold[:], T.ym[:], 0.0, A.add, A.min, ["hold", "ym"], ["yh"])
        ts(T.ids[:], T.yh[:, 15:CAP:16], 0.25, None, A.add, None, ["yh"], ["ids"])
        if not last:
            dma("y", T.ya[:, 0:CAP], T.pay[:, V:VP], ["pay4"], ["ya"])
            dma("y", T.yb[:, 0:CAP], T.pay[:, V:VP], ["pay4"], ["yb"])
        cp(T.nbu[:], T.nbi[:].indirect(T.ids[:]), ["nbi", "nbp", "ids"], ["nbu"])
        for h in range(2):
            act(T.rn[:, h:2 * CAP:2], T.ndt[:].indirect(T.ids[:]), F.Identity, ["ndt", "ndp", "ids", "mk0", "mk1"],
                ["rn%d" % h], scale=T.mk[:, h:h + 1])
        if r == 0:
            late_constants()
            cp(T.labf[:, 0:V], T.labi[:], ["labi"], ["labf"])
            dma("y", T.labf[15:128:16, 0:V], T.pay[0:8, 0:V], PAY, ["labf"])
            late_vector()
            late_dmas()
        if r == 1:
            clear_flags()

        def gather(q, arr, u):
            src, dst = (T.nbu, T.gn) if arr == "n" else (T.labu, T.gl)
            o = dst[:, 16 * UC * u:16 * UC * (u + 1)]
            i_ = w[:].indirect(src[:, UC * u:UC * (u + 1)])
            R = WK + ["nbu" if arr == "n" else "labu"]
            if q == "v":
                cp(o, i_, R, ["g%s%d" % (arr, u)])
            else:
                act(o, i_, F.Copy, R, ["g%s%d" % (arr, u)])

        def diffs(arr, u, slot):
            rs = T.rn if arr == "n" else T.rl
            R = ["r%s0" % arr, "r%s1" % arr] + DM
            for bnk in range(2):
                p0 = 1024 * slot + 512 * bnk
                c0 = 2 * UC * u + 64 * bnk
                for ii in range(1, 8):
                    mm(T.pd[:, p0 + ii:p0 + 512:8], T.dmx[:, 128 * ii:128 * ii + 128], rs[:, c0:c0 + 64], True, True,
                       R, ["pd%d" % slot])
                mm(T.pd[:, p0 + 8:p0 + 512:16], T.dmx[:, 1024:1152], rs[:, c0:c0 + 64:2], True, False, R, ["pd%d" % slot])
                mm(T.pd[:, p0 + 8:p0 + 512:16], T.dmx[:, 0:128], rs[:, c0 + 1:c0 + 64:2], False, True, R, ["pd%d" % slot])

        def least(arr, u, slot):
            gsrc, o = (T.gn, T.on) if arr == "n" else (T.gl, T.ol)
            a, b = 16 * UC * u, 16 * UC * (u + 1)
            scan(o[:, a:b], T.pd[:, 1024 * slot:1024 * slot + 1024], gsrc[:, a:b], 0.0, A.add, A.min,
                 ["g%s%d" % (arr, u)], ["o%s%d" % (arr, u)], ["pd%d" % slot])

        def lengths():
            for h in range(2):
                tab, keys = (T.lda, ["lda", "ldap"]) if h == 0 or r == 0 else (T.ldb, ["ldb", "ldbp"])
                act(T.rl[:, h:2 * CAP:2], tab[:].indirect(T.ids[:]), F.Identity, keys + ["ids", "mk0", "mk2"],
                    ["rl%d" % h], scale=T.mk[:, 2 * h:2 * h + 1])

        def labels():
            cp(T.labu[:], T.labf[:].indirect(T.ids[:]), ["labf", "labp", "ids"], ["labu"])

        units = [("n", u) for u in range(NU)] + [("l", u) for u in range(NU)]
        ON = ["on%d" % u for u in range(NU)]
        OL = ["ol%d" % u for u in range(NU)]
        GL = ["gl%d" % u for u in range(NU)]
        sn = T.on[:, 15:16 * CAP:16]
        e7 = T.dmx[:, 1024:1152]
        gather("v", "n", 0)
        if r > 0:
            labels()
        for u in range(VUNITS, NU - 1):
            gather("s", "n", u)
        lengths()
        gather("s", "n", NU - 1)
        for k, (arr, u) in enumerate(units):
            diffs(arr, u, k % 2)
            if 0 < k < VUNITS:
                gather("v", arr, u)
            if k == 1 and r == 0:
                labels()
            if k == 1:
                for x in range(NU):
                    gather("s", "l", x)
            least(arr, u, k % 2)
            if k == NU + 1:
                mm(T.pc[:, 0:CAP], T.idn[:], sn, True, False, ON + ["idn"], ["pc"])
                mm(T.pc[:, 0:CAP], e7, T.rn[:, 1:2 * CAP:2], False, True, ["rn1"] + DM, ["pc"])
                mm(T.pk[:, 0:CAP], T.idn[:], sn, True, False, ON + ["idn"], ["pk"])
                mm(T.pk[:, 0:CAP], e7, T.rn[:, 1:2 * CAP:2], False, False, ["rn1"] + DM, ["pk"])
                mm(T.pk[:, 0:CAP], T.one[0:1, :], T.rc[0:1, :], False, False, ["one", "rc"], ["pk"])
                if not last:
                    mm(T.pv[:, 0:CAP], T.one[0:1, :], T.ra[0:1, :], True, False, ["one", "ra"], ["pv"])
                    mm(T.pv[:, 0:CAP], T.one[0:1, :], T.rb[0:1, :], False, False, ["one", "rb"], ["pv"])
        tt(T.up[:], T.pc[:, 0:CAP], T.ol[:, 15:16 * CAP:16], A.is_lt, OL, ["up"], ["pc"])
        if not last:
            mm(T.pv[:, 0:CAP], T.nbk[:], T.up[:], False, True, ["up", "nbk"], ["pv"])
        mm(T.pk[:, 0:CAP], T.nid[:], T.up[:], False, True, ["up", "nid"], ["pk"])

        def new_d():
            tt(T.newd[:], T.pk[:, 0:CAP], T.gl[:, 15:16 * CAP:16], A.min, GL, ["newd"], ["pk"])
            cp(T.dm[:].indirect(T.ids[:]), T.newd[:], ["newd", "ids"], ["dm", "dmp"])

        def new_labels():
            col = 13 + r
            tr32(T.kt[:], T.pk[:, 0:CAP], [], ["kt"], ["pk"])
            scan(T.ks[:], T.kd[:], T.kt[:], 0.0, A.add, A.min, ["kd", "kt"], ["ks"])
            res = T.ks[:, 15:CAP:16]
            ts(T.ki[:], res, 16.0, 15.0, A.mult, A.add, ["ks"], ["ki"])
            ts(T.kh[:], res, 1024.0, None, A.is_lt, None, ["ks"], ["kh"])
            ts(T.km[:], T.ki[:], 15, None, A.bitwise_and, None, ["ki"], ["km"])
            if not last:
                ts(T.kc[:], T.ki[:], 4, None, A.arith_shift_right, None, ["ki"], ["kc"])
            ts(T.kf[:], T.km[:], -16.0, None, A.add, None, ["km"], ["kf"])
            if not last:
                ts(T.zd[:, col:CAP:16], T.kc[:], 255.0, -255.0, A.min, A.add, ["kc"], ["zd"])
            tt(T.zl[:, col:CAP:16], T.kf[:], T.kh[:], A.mult, ["kf", "kh"], ["zl"])
            if not last:
                tr32(T.dd[:], T.zd[:], ["zd"], ["dd"])
            tr32(T.dl[:], T.zl[:], ["zl"], ["dl"])
            if last:
                ts(T.zt[:].indirect(T.ids[:]), T.dl[:], 1.0, float(NONE), A.mult, A.add, ["dl", "ids"], ["zt"])
                return
            cp(T.labt[:], T.labu[:], ["labu"], ["labt"])
            tt(T.ldb[:].indirect(T.ids[:]), T.rl[:, 1:2 * CAP:2], T.dd[:], A.add, ["rl1", "dd", "ids"], ["ldb", "ldbp"])
            tt(T.labf[:].indirect(T.ids[:]), T.labt[:], T.dl[:], A.add, ["labt", "dl", "ids"], ["labf", "labp"])
            fill(T.zd[:, col:CAP:16], 0.0, "zd")
            fill(T.zl[:, col:CAP:16], 0.0, "zl")

        if last:
            new_d()
            dma("y", T.yd[:], T.dm[:, 0:V], ["dm"], ["yd"])
            new_labels()
            dma("s", T.yl[15:128:16, :], T.zt[15:128:16, 0:V], ["zt"], ["yl"])
            break
        cp(T.nbf[:], T.nbu[:], ["nbu"], ["nbf"])
        tt(T.xx[:, 0:CAP], T.pv[:, 0:CAP], T.nbf[:], A.max, ["nbf"], ["xa"], ["pv"])
        tt(T.xx[:, CAP:CAP + 16], T.pv[:, 0:16], T.nbf[:, 0:16], A.max, ["nbf"], ["xb"], ["pv"])
        tr32(T.tx[:, 0:CAP], T.xx[:, 0:CAP], ["xa"], ["ta1"])
        tr32(T.tx[:, CAP:2 * CAP], T.xx[:, 16:CAP + 16], ["xa", "xb"], ["ta2"])
        cp(T.lst[:], T.tx[:].indirect(T.sl[:]), ["ta1", "ta2", "sl"], ["lst"])
        for i in range(VPUSH, 16):
            act(fa[:].indirect(T.lst[:, 24 * i:24 * i + 24]), T.caf[:], F.Silu, ["lst", "caf"], ka)
        new_d()
        dma("y", W_[r + 1][:, 0:V], T.dm[:, 0:V], ["dm"], ["w%do" % (r + 1)])
        for i in range(VPUSH):
            cp(fv[:].indirect(T.lst[:, 24 * i:24 * i + 24]), T.cvb[:], ["lst", "cvb"], kv)
        act(SD[r + 1][:], T.dm[:, 0:V].indirect(T.sndu[:]), F.Copy, ["dm", "sndu"], ["sd%d" % (r + 1)])
        scan(T.ex[:, 16:16 + NG], fv[:, V:V + NG], fa[:, V:V + NG], 0.0, A.add, A.add, kv + ka, ["ex"])
        tt(T.t1[:], T.ex[:, 31:16 + NG:16], T.ex[:, 15:NG:16], A.subtract, ["ex", "ex0"], ["t1"])
        ts(FS[r][:], T.t1[:], THR, float(V), A.is_lt, A.mult, ["t1"], ["fs%d" % r])
        exchange(lambda d: FS[r][:, 14 * (d - 1):14 * d], lambda d: FR[r][:, 14 * (d - 1):14 * d], -1,
                 "af%d" % r, "lf%d" % r, ["fs%d" % r], ["fr%d" % r])
        send_d(r + 1, ["sd%d" % (r + 1)])
        new_labels()
        if r == RO - 2:
            dma("y", T.yl[:], T.labf[:, 0:V], ["labf"], ["yl"])
        ts(T.ta[:], T.cum[:], CAP - 0.5, -THR, A.is_gt, A.mult, ["cum"], ["ta"])
        tt(T.tb[:], T.ta[:], f_, A.mult, ["ta"] + FK, ["tb"])
        ts(T.thr[:], T.tb[:], THR, None, A.add, None, ["tb"], ["thr"])
        tt(T.bo[:], FR[r][:], T.sndf[:], A.add, ["fr%d" % r, "sndf"], ["bo"])
        cp(T.bu[:], T.bo[:], ["bo"], ["bu"])
        for d in range(VBACK, NR - 1):
            act(fa[:, 0:2 * V].indirect(T.bu[:, 14 * d:14 * d + 14]), T.caf[:, 0:GS], F.Silu, ["bu", "caf"], ka)
        for d in range(VBACK):
            cp(fv[:, 0:2 * V].indirect(T.bu[:, 14 * d:14 * d + 14]), T.cvb[:, 0:GS], ["bu", "cvb"], kv)
        scan(T.ex[:, 16:16 + V], fv[:, 0:V], fa[:, 0:V], 0.0, A.add, A.add, kv + ka, ["ex"])
        tt(T.t1[:, 0:96], T.ex[:, 31:16 + V:16], T.ex[:, 15:V:16], A.subtract, ["ex", "ex0"], ["t1"])
        tt(f_, T.t1[:, 0:96], T.thr[:], A.is_gt, ["t1", "thr"], FK)

    for sem, val in cnt.items():
        need("g", (sem, val, {}))
